import numpy as np
CORES = [2,3,4,5,6]
N = 5
ROOT = 2
def setup_inputs(rng):
    return {"x": rng.standard_normal((N, 128, 64), dtype=np.float32)}
def reference(x):
    return {"y": np.broadcast_to(x[ROOT], x.shape)}

from concourse.bass import DstId, RemoteDMATransfer

SCRATCH = {
    "stage": ("sbuf", [128, 64], "float32"),
    "land": ("sbuf", [128, 64], "float32"),
}
SEMAPHORES = ["loaded", "read", "arrived", "stored"]

ENGINES = 16


def rank_program(g, core, T, topo):
    rank = T.rank_of(core)
    if rank is None:
        return

    root_core = T.cores[T.root]

    if core == root_core:
        g.dma_start(T.stage[:], T.x[:]).then_inc(T.sem.loaded, 16)
        g.dma_start(T.y[:], T.x[:]).then_inc(T.sem.stored, 16)
        g.wait_ge(T.sem.loaded, 16)

        peers = [c for c in T.cores if c != core]
        ids = []
        for c in peers:
            a = topo.addr(c)
            ids.append(DstId(rid=a[0], pnc=a[1]))
        g.remote_dma_fused(
            [
                RemoteDMATransfer(
                    dst_ids=ids,
                    dma_engine_mask=topo.mask(core, peers[0]),
                    remote_sem=T.sem.arrived,
                    srcs=[T.stage[:]],
                    dsts=[T.land[:] for c in peers],
                    alu_op=0,
                )
            ],
            local_sem=T.sem.read,
        )
        g.wait_ge(T.sem.read, ENGINES)
        g.wait_ge(T.sem.stored, 16)
    else:
        g.wait_ge(T.sem.arrived, ENGINES)
        g.dma_start(T.y[:], T.land[:]).then_inc(T.sem.stored, 16)
        g.wait_ge(T.sem.stored, 16)
